import numpy as np, ml_dtypes
CORES = [9,41,49,65,73,81,97,113,15,47,55,71,79,87,103,119]
N = 16
NB, B = 3, 512
def setup_inputs(rng):
    return {"x": rng.standard_normal((N, 128, NB * B), dtype=np.float32).astype(ml_dtypes.bfloat16), "wv": (rng.standard_normal((N, 128, 128), dtype=np.float32) / 16).astype(ml_dtypes.bfloat16), "wh": (rng.standard_normal((N, 128, 128), dtype=np.float32) / 16).astype(ml_dtypes.bfloat16)}
def setup_inputs_big(rng):
    d = setup_inputs(rng)
    for k in ("x",): d[k] = (d[k].astype(np.float32) * 1048576.0).astype(d[k].dtype)
    return d
def setup_inputs_small(rng):
    d = setup_inputs(rng)
    for k in ("x",): d[k] = (d[k].astype(np.float32) * (1 / 1048576.0)).astype(d[k].dtype)
    return d
def setup_inputs_apart(rng):
    d = setup_inputs(rng)
    f = (10.0 ** rng.permutation(np.linspace(-1.5, 1.5, N))).astype(np.float32).reshape(N, 1, 1)
    for k in ("x",): d[k] = (d[k].astype(np.float32) * f).astype(d[k].dtype)
    return d
def reference(x, wv, wh):
    X, WV, WH = x.astype(np.float64), wv.astype(np.float64), wh.astype(np.float64)
    h = np.zeros((N, NB, 128, B))
    for r in range(N):
        for c in range(NB):
            a = X[r][:, B * c:B * c + B].copy()
            if r: a += WV[r].T @ h[r - 1][c]
            if c: a += WH[r].T @ h[r][c - 1]
            h[r][c] = np.maximum(a, 0.0)
    return {"y": np.concatenate([h[:, c] for c in range(NB)], axis=2).astype(ml_dtypes.bfloat16)}

@@ -1,0 +1,331 @@
+from concourse.bass import DstId, RemoteDMATransfer
+from concourse.mybir import AluOpType
+
+NB, B = 3, 512
+STAGES = [(0, 2, 1, 4, 2), (2, 9, 4, 2, 2), (9, 16, 4, 2, 2)]
+NMAX = max(hi - lo for lo, hi, _p, _s, _g in STAGES)
+SMAX = max(st[3] for st in STAGES)
+XCOLS = max((hi - lo) * NB * (B // p) for lo, hi, p, _s, _g in STAGES)
+HINW = max([B // st[2] for st in STAGES[1:]] + [1])
+ZW = max(B // st[2] // st[3] for st in STAGES)
+NREL = 2
+NBANK = 8
+
+SCRATCH = {
+    "Wl": ("sbuf", [128, 256], "bfloat16"),
+    "X": ("sbuf", [128, NB * B], "bfloat16"),
+    "YD": ("sbuf", [128, NB * B], "bfloat16"),
+    "Wb": ("sbuf", [128, NMAX * 256], "bfloat16"),
+    "Xb": ("sbuf", [128, XCOLS], "bfloat16"),
+    "Hb": ("sbuf", [128, XCOLS], "bfloat16"),
+    "Hin": ("sbuf", [128, NB * HINW], "bfloat16"),
+    "idsrc": ("sbuf", [128, 129], "bfloat16"),
+    "idd": ("dram", [129, 128], "bfloat16"),
+    "ident": ("sbuf", [128, 128], "bfloat16"),
+    "zero": ("sbuf", [128, ZW], "float32"),
+}
+for _b in range(NBANK):
+    SCRATCH["ps%d" % _b] = ("psum", [128, 512], "float32")
+
+SEMAPHORES = (["wl", "st", "ls", "rw", "cz", "ci", "id1", "id2"]
+              + ["%s%d" % (a, c) for a in ("xl", "rx", "y", "h") for c in range(NB)]
+              + ["w%d" % i for i in range(NMAX)]
+              + ["x%d_%d" % (i, c) for i in range(NMAX) for c in range(NB)]
+              + ["%s%d_%d" % (a, c, q) for a in ("t", "v") for c in range(NB) for q in range(SMAX)])
+
+_CACHE = {}
+
+
+def _bits(topo, src, dsts):
+    m = -1
+    for d in dsts:
+        m &= topo.mask(src, d)
+    return [b for b in range(64) if (m >> b) & 1]
+
+
+def _split(bits, m):
+    per = 1
+    while per * 2 * m <= len(bits):
+        per *= 2
+    return [sum(1 << b for b in bits[j * per:(j + 1) * per]) for j in range(m)], per
+
+
+def _plan(T, topo):
+    if "p" in _CACHE:
+        return _CACHE["p"]
+    allc = list(range(topo.CHIPS * topo.CORES_PER_CHIP))
+    ranks = list(T.cores)
+    used = set(ranks)
+    free = [c for c in allc if all(topo.may_write(c, d) for d in allc if d != c)]
+    chips = sorted(set(topo.chip(c) for c in allc))
+    on = {ch: [c for c in allc if topo.chip(c) == ch] for ch in chips}
+
+    def pick(ch, die):
+        cand = [c for c in on[ch] if c in free and c not in used]
+        cand.sort(key=lambda c: (topo.die(c) != die, c))
+        return cand[0] if cand else None
+
+    cores = []
+    for s, (lo, hi, P, _S, _G) in enumerate(STAGES):
+        mine = ranks[lo:hi]
+        die = topo.die(mine[0])
+        prev = [topo.chip(c) for c in cores[-1]] if s and STAGES[s - 1][2] == P else []
+
+        def key(ch):
+            direct = sum(1 for r in mine if all(topo.may_write(r, c) for c in on[ch] if c != r))
+            nr = sum(1 for c in on[ch] if c in ranks)
+            home = sum(1 for c in on[ch] if c in mine)
+            return (-direct, ch not in prev, -home if P == 1 else nr, ch)
+        order = sorted(chips, key=key)
+        if prev and all(ch in order[:P] for ch in prev):
+            order = prev
+        got = []
+        for ch in order:
+            if len(got) == P:
+                break
+            c = pick(ch, die)
+            if c is not None:
+                got.append(c)
+                used.add(c)
+        cores.append(got)
+    send, relay_of = {}, {}
+    for s, (lo, hi, P, _S, _G) in enumerate(STAGES):
+        for r in range(lo, hi):
+            rc = ranks[r]
+            if all(topo.may_write(rc, c) for c in cores[s]):
+                send[r] = [(rc, list(range(P)))]
+                continue
+            rel = [c for c in on[topo.chip(rc)] if c in free and c not in used]
+            rel.sort(key=lambda c: (topo.die(c) != topo.die(rc), c))
+            nrel = NREL if len(rel) >= NREL and P % NREL == 0 else 1
+            rel = rel[:nrel]
+            used.update(rel)
+            share = P // nrel
+            send[r] = [(c, list(range(j * share, (j + 1) * share))) for j, c in enumerate(rel)]
+            for j, c in enumerate(rel):
+                relay_of[c] = (r, j)
+    pl = {"ranks": ranks, "cores": cores, "send": send, "relay_of": relay_of,
+          "stage_of": {r: s for s, st in enumerate(STAGES) for r in range(st[0], st[1])}}
+    _CACHE["p"] = pl
+    return pl
+
+
+def _did(topo, c):
+    rid, pid, _se = topo.addr(c)
+    return DstId(rid=rid, pnc=pid)
+
+
+def _in_eng(topo, pl, r, k):
+    cs = pl["cores"][pl["stage_of"][r]]
+    for src, ks in pl["send"][r]:
+        if k in ks:
+            bits = _bits(topo, src, [cs[j] for j in ks])
+            return _split(bits, 1)[1], _split(bits, len(ks))[1]
+
+
+def _groups(s):
+    lo, hi, _P, _S, G = STAGES[s]
+    n = hi - lo
+    return [list(range(a, min(a + G, n))) for a in range(0, n, G)]
+
+
+def _ret_masks(topo, pl, s, k, grp):
+    lo = STAGES[s][0]
+    bits = _bits(topo, pl["cores"][s][k], [pl["ranks"][lo + i] for i in grp])
+    return _split(bits, len(grp))
+
+
+def _fwd_masks(topo, pl, s, k):
+    ratio = STAGES[s + 1][2] // STAGES[s][2]
+    src = pl["cores"][s][k]
+    dsts = pl["cores"][s + 1][k * ratio:(k + 1) * ratio]
+    bits = _bits(topo, src, dsts)
+    busy = _bits(topo, src, [c for c in pl["ranks"] if c != src])
+    spare = [b for b in bits if b not in busy]
+    masks, per = _split(spare if len(spare) >= ratio else bits, ratio)
+    return dsts, masks, per
+
+
+def _inflow(g, T, topo, pl, src, r, ks, waits, ls):
+    s = pl["stage_of"][r]
+    lo, _hi, P, _S, _G = STAGES[s]
+    i, w = r - lo, B // P
+    cs = [pl["cores"][s][k] for k in ks]
+    bits = _bits(topo, src, cs)
+    for what in ([0, "w", 1, 2] if r == 0 else ["w", 0, 1, 2]):
+        g.wait_ge(*waits[what])
+        if what == "w":
+            masks, per = _split(bits, 1)
+            tr = [RemoteDMATransfer(dst_ids=[_did(topo, c) for c in cs], dma_engine_mask=masks[0],
+                                    remote_sem=T.sem["w%d" % i], srcs=[T.Wl[:, :]],
+                                    dsts=[T.Wb[:, i * 256:(i + 1) * 256] for _c in cs])]
+            ls[0] += per
+        else:
+            c = what
+            masks, per = _split(bits, len(ks))
+            o = (i * NB + c) * w
+            tr = [RemoteDMATransfer(dst_ids=[_did(topo, cs[j])], dma_engine_mask=masks[j],
+                                    remote_sem=T.sem["x%d_%d" % (i, c)],
+                                    src=T.X[:, c * B + k * w:c * B + (k + 1) * w], dst=T.Xb[:, o:o + w])
+                  for j, k in enumerate(ks)]
+            ls[0] += per * len(ks)
+        g.remote_dma_fused(tr, local_sem=T.sem.ls)
+
+
+def _rank_prog(g, core, T, topo, pl, r):
+    sem = T.sem
+    s = pl["stage_of"][r]
+    lo, _hi, P, _S, _G = STAGES[s]
+    ls = [0]
+    for c in range(NB):
+        g.sync.dma_start(T.X[:, c * B:(c + 1) * B], T.x[:, c * B:(c + 1) * B]).then_inc(sem["xl%d" % c], 16)
+    g.scalar.dma_start(T.Wl[:, 0:128], T.wv[:, :]).then_inc(sem.wl, 16)
+    g.scalar.dma_start(T.Wl[:, 128:256], T.wh[:, :]).then_inc(sem.wl, 16)
+    waits = {"w": (sem.wl, 32)}
+    for c in range(NB):
+        waits[c] = (sem["xl%d" % c], 16)
+    if pl["send"][r][0][0] == core:
+        _inflow(g, T, topo, pl, core, r, pl["send"][r][0][1], waits, ls)
+    else:
+        rel = [c for c, _ks in pl["send"][r]]
+        masks, per = _split(_bits(topo, core, rel), 1)
+        ids = [_did(topo, c) for c in rel]
+        for what in ["w", 0, 1, 2]:
+            g.wait_ge(*waits[what])
+            ap = T.Wl[:, :] if what == "w" else T.X[:, what * B:(what + 1) * B]
+            g.remote_dma_fused([RemoteDMATransfer(dst_ids=ids, dma_engine_mask=masks[0],
+                                                  remote_sem=sem.rw if what == "w" else sem["rx%d" % what],
+                                                  srcs=[ap], dsts=[ap for _c in rel])], local_sem=sem.ls)
+            ls[0] += per
+    i = r - lo
+    grp = [gr for gr in _groups(s) if i in gr][0]
+    total = sum(_ret_masks(topo, pl, s, k, grp)[1] for k in range(P))
+    for c in range(NB):
+        g.sync.wait_ge(sem["y%d" % c], total)
+        g.sync.dma_start(T.y[:, c * B:(c + 1) * B], T.YD[:, c * B:(c + 1) * B]).then_inc(sem.st, 16)
+    g.sync.wait_ge(sem.st, 16 * NB)
+    g.wait_ge(sem.ls, ls[0])
+
+
+def _relay_prog(g, core, T, topo, pl):
+    r, j = pl["relay_of"][core]
+    rel = [c for c, _ks in pl["send"][r]]
+    per = _split(_bits(topo, pl["ranks"][r], rel), 1)[1]
+    waits = {"w": (T.sem.rw, per)}
+    for c in range(NB):
+        waits[c] = (T.sem["rx%d" % c], per)
+    ls = [0]
+    _inflow(g, T, topo, pl, core, r, pl["send"][r][j][1], waits, ls)
+    g.wait_ge(T.sem.ls, ls[0])
+
+
+def _compute_prog(g, core, T, topo, pl, s, k):
+    sem = T.sem
+    lo, hi, P, S, _G = STAGES[s]
+    n, w = hi - lo, B // P
+    wq = w // S
+    te, ve = g.tensor, g.vector
+    ve.memset(T.zero[:, :], 0.0).then_inc(sem.cz, 1)
+    ve.memset(T.idsrc[:, 1:129], 0.0).then_inc(sem.ci, 1)
+    ve.memset(T.idsrc[:, 0:1], 1.0).then_inc(sem.ci, 1)
+    g.sync.wait_ge(sem.ci, 2)
+    g.sync.dma_start(T.idd[:, :], T.idsrc[:, :]).then_inc(sem.id1, 16)
+    g.sync.wait_ge(sem.id1, 16)
+    g.sync.dma_start(T.ident[:, :], T.idd[0:128, :]).then_inc(sem.id2, 16)
+    te.wait_ge(sem.id2, 16)
+    ve.wait_ge(sem.cz, 1)
+
+    J = [(c, i, q) for c in range(NB) for i in range(n) for q in range(S)]
+    seen = set()
+
+    def twait(name, val):
+        if (name, val) not in seen:
+            seen.add((name, val))
+            te.wait_ge(sem[name], val)
+
+    def off(i, c, q):
+        return (i * NB + c) * w + q * wq
+
+    def ps(j):
+        return T["ps%d" % (j % NBANK)][:, 0:wq]
+
+    def pre(j):
+        c, i, q = J[j]
+        crit = lo + i > 0
+        if j >= NBANK:
+            c0, i0, q0 = J[j - NBANK]
+            twait("v%d_%d" % (c0, q0), i0 + 1)
+        twait("x%d_%d" % (i, c), _in_eng(topo, pl, lo + i, k)[1])
+        o = off(i, c, q)
+        last = te.matmul(ps(j), T.ident[:, :], T.Xb[:, o:o + wq], True, not (crit or c > 0))
+        if c > 0:
+            twait("w%d" % i, _in_eng(topo, pl, lo + i, k)[0])
+            twait("v%d_%d" % (c - 1, q), i + 1)
+            o = off(i, c - 1, q)
+            last = te.matmul(ps(j), T.Wb[:, i * 256 + 128:i * 256 + 256], T.Hb[:, o:o + wq], False, not crit)
+        if not crit:
+            last.then_inc(sem["t%d_%d" % (c, q)], 1)
+
+    def crit(j):
+        c, i, q = J[j]
+        if lo + i == 0:
+            return
+        twait("w%d" % i, _in_eng(topo, pl, lo + i, k)[0])
+        if i > 0:
+            twait("v%d_%d" % (c, q), i)
+            o = off(i - 1, c, q)
+            rhs = T.Hb[:, o:o + wq]
+        else:
+            ratio = P // STAGES[s - 1][2]
+            twait("h%d" % c, _fwd_masks(topo, pl, s - 1, k // ratio)[2])
+            rhs = T.Hin[:, c * w + q * wq:c * w + (q + 1) * wq]
+        te.matmul(ps(j), T.Wb[:, i * 256:i * 256 + 128], rhs, False, True).then_inc(sem["t%d_%d" % (c, q)], 1)
+
+    pre(0)
+    for j in range(len(J)):
+        crit(j)
+        if j + 1 < len(J):
+            pre(j + 1)
+    for j, (c, i, q) in enumerate(J):
+        ve.wait_ge(sem["t%d_%d" % (c, q)], i + 1)
+        o = off(i, c, q)
+        ve.tensor_tensor(T.Hb[:, o:o + wq], ps(j), T.zero[:, 0:wq], AluOpType.max).then_inc(sem["v%d_%d" % (c, q)], 1)
+
+    ls = 0
+    for c in range(NB):
+        for grp in _groups(s):
+            for q in range(S):
+                g.wait_ge(sem["v%d_%d" % (c, q)], grp[-1] + 1)
+            if grp[-1] == n - 1 and s + 1 < len(STAGES):
+                dsts, masks, per = _fwd_masks(topo, pl, s, k)
+                w2 = B // STAGES[s + 1][2]
+                o = off(n - 1, c, 0)
+                g.remote_dma_fused([RemoteDMATransfer(dst_ids=[_did(topo, d)], dma_engine_mask=masks[jj],
+                                                      remote_sem=sem["h%d" % c],
+                                                      src=T.Hb[:, o + jj * w2:o + (jj + 1) * w2],
+                                                      dst=T.Hin[:, c * w2:(c + 1) * w2])
+                                    for jj, d in enumerate(dsts)], local_sem=sem.ls)
+                ls += per * len(dsts)
+            masks, per = _ret_masks(topo, pl, s, k, grp)
+            g.remote_dma_fused([RemoteDMATransfer(dst_ids=[_did(topo, pl["ranks"][lo + i])],
+                                                  dma_engine_mask=masks[jj], remote_sem=sem["y%d" % c],
+                                                  src=T.Hb[:, off(i, c, 0):off(i, c, 0) + w],
+                                                  dst=T.YD[:, c * B + k * w:c * B + (k + 1) * w])
+                                for jj, i in enumerate(grp)], local_sem=sem.ls)
+            ls += per * len(grp)
+    g.wait_ge(sem.ls, ls)
+
+
+def rank_program(g, core, T, topo):
+    pl = _plan(T, topo)
+    rank = T.rank_of(core)
+    if rank is not None:
+        _rank_prog(g, core, T, topo, pl, rank)
+        return
+    if core in pl["relay_of"]:
+        _relay_prog(g, core, T, topo, pl)
+        return
+    for s, cs in enumerate(pl["cores"]):
+        if core in cs:
+            _compute_prog(g, core, T, topo, pl, s, cs.index(core))
+            return

@@ -2,36 +2,32 @@ from concourse.bass import DstId, RemoteDMATransfer
 from concourse.mybir import AluOpType
 
 NB, B = 3, 512
-STAGES = [(0, 2, 1, 4, 2), (2, 9, 4, 2, 2), (9, 16, 4, 2, 2)]
-NMAX = max(hi - lo for lo, hi, _p, _s, _g in STAGES)
-SMAX = max(st[3] for st in STAGES)
-XCOLS = max((hi - lo) * NB * (B // p) for lo, hi, p, _s, _g in STAGES)
-HINW = max([B // st[2] for st in STAGES[1:]] + [1])
-ZW = max(B // st[2] // st[3] for st in STAGES)
+N = 16
+P = 8
+W = B // P
 NREL = 2
 NBANK = 8
+ND = N - 2
 
 SCRATCH = {
     "Wl": ("sbuf", [128, 256], "bfloat16"),
     "X": ("sbuf", [128, NB * B], "bfloat16"),
     "YD": ("sbuf", [128, NB * B], "bfloat16"),
-    "Wb": ("sbuf", [128, NMAX * 256], "bfloat16"),
-    "Xb": ("sbuf", [128, XCOLS], "bfloat16"),
-    "Hb": ("sbuf", [128, XCOLS], "bfloat16"),
-    "Hin": ("sbuf", [128, NB * HINW], "bfloat16"),
+    "Wb": ("sbuf", [128, N * 256], "bfloat16"),
+    "Xb": ("sbuf", [128, N * NB * W], "bfloat16"),
+    "Hb": ("sbuf", [128, N * NB * W], "bfloat16"),
     "idsrc": ("sbuf", [128, 129], "bfloat16"),
     "idd": ("dram", [129, 128], "bfloat16"),
     "ident": ("sbuf", [128, 128], "bfloat16"),
-    "zero": ("sbuf", [128, ZW], "float32"),
+    "zero": ("sbuf", [128, W], "float32"),
 }
 for _b in range(NBANK):
     SCRATCH["ps%d" % _b] = ("psum", [128, 512], "float32")
 
 SEMAPHORES = (["wl", "st", "ls", "rw", "cz", "ci", "id1", "id2"]
-              + ["%s%d" % (a, c) for a in ("xl", "rx", "y", "h") for c in range(NB)]
-              + ["w%d" % i for i in range(NMAX)]
-              + ["x%d_%d" % (i, c) for i in range(NMAX) for c in range(NB)]
-              + ["%s%d_%d" % (a, c, q) for a in ("t", "v") for c in range(NB) for q in range(SMAX)])
+              + ["%s%d" % (a, c) for a in ("xl", "rx", "y", "t", "v") for c in range(NB)]
+              + ["w%d" % i for i in range(N)] + ["g%d" % i for i in range(N)]
+              + ["x%d_%d" % (i, c) for i in range(N) for c in range(NB)])
 
 _CACHE = {}
 
@@ -59,53 +55,46 @@ def _plan(T, topo):
     free = [c for c in allc if all(topo.may_write(c, d) for d in allc if d != c)]
     chips = sorted(set(topo.chip(c) for c in allc))
     on = {ch: [c for c in allc if topo.chip(c) == ch] for ch in chips}
-
-    def pick(ch, die):
-        cand = [c for c in on[ch] if c in free and c not in used]
-        cand.sort(key=lambda c: (topo.die(c) != die, c))
-        return cand[0] if cand else None
-
+    dies = sorted(set(topo.die(c) for c in allc))
     cores = []
-    for s, (lo, hi, P, _S, _G) in enumerate(STAGES):
-        mine = ranks[lo:hi]
-        die = topo.die(mine[0])
-        prev = [topo.chip(c) for c in cores[-1]] if s and STAGES[s - 1][2] == P else []
-
-        def key(ch):
-            direct = sum(1 for r in mine if all(topo.may_write(r, c) for c in on[ch] if c != r))
-            nr = sum(1 for c in on[ch] if c in ranks)
-            home = sum(1 for c in on[ch] if c in mine)
-            return (-direct, ch not in prev, -home if P == 1 else nr, ch)
-        order = sorted(chips, key=key)
-        if prev and all(ch in order[:P] for ch in prev):
-            order = prev
-        got = []
-        for ch in order:
-            if len(got) == P:
-                break
-            c = pick(ch, die)
-            if c is not None:
-                got.append(c)
-                used.add(c)
-        cores.append(got)
+    for ch in sorted(chips, key=lambda ch: (sum(1 for c in on[ch] if c in ranks), ch)):
+        if len(cores) == P:
+            break
+        want = dies[len(cores) % len(dies)]
+        cand = [c for c in on[ch] if c in free and c not in used]
+        cand.sort(key=lambda c: (topo.die(c) != want, c))
+        if cand:
+            cores.append(cand[0])
+            used.add(cand[0])
     send, relay_of = {}, {}
-    for s, (lo, hi, P, _S, _G) in enumerate(STAGES):
-        for r in range(lo, hi):
-            rc = ranks[r]
-            if all(topo.may_write(rc, c) for c in cores[s]):
-                send[r] = [(rc, list(range(P)))]
-                continue
-            rel = [c for c in on[topo.chip(rc)] if c in free and c not in used]
-            rel.sort(key=lambda c: (topo.die(c) != topo.die(rc), c))
-            nrel = NREL if len(rel) >= NREL and P % NREL == 0 else 1
-            rel = rel[:nrel]
-            used.update(rel)
-            share = P // nrel
-            send[r] = [(c, list(range(j * share, (j + 1) * share))) for j, c in enumerate(rel)]
-            for j, c in enumerate(rel):
+    for r, rc in enumerate(ranks):
+        hel = [c for c in on[topo.chip(rc)] if c not in used and topo.die(c) == topo.die(rc)]
+        hel.sort(key=lambda c: (-sum(1 for x in cores if topo.may_write(c, x)), c))
+        snd = [rc] + hel[:NREL]
+        load = {c: [] for c in snd}
+        for k in sorted(range(P), key=lambda k: (sum(1 for c in snd if topo.may_write(c, cores[k])), k)):
+            cand = [c for c in snd if topo.may_write(c, cores[k])]
+            load[min(cand, key=lambda c: (len(load[c]), snd.index(c)))].append(k)
+        send[r] = [(c, sorted(load[c])) for c in snd if load[c]]
+        for j, (c, _ks) in enumerate(send[r]):
+            if c != rc:
+                used.add(c)
                 relay_of[c] = (r, j)
-    pl = {"ranks": ranks, "cores": cores, "send": send, "relay_of": relay_of,
-          "stage_of": {r: s for s, st in enumerate(STAGES) for r in range(st[0], st[1])}}
+    rh, rh_of = [], {}
+    for k, cc in enumerate(cores):
+        idle = [c for c in on[topo.chip(cc)] if c not in used]
+        load = {c: [] for c in idle}
+        rh.append({})
+        for i in range(ND):
+            cand = [c for c in idle if topo.may_write(c, ranks[i])]
+            h = min(cand, key=lambda c: (len(load[c]), sum(1 for x in ranks if topo.may_write(c, x)), c))
+            load[h].append(i)
+            rh[k][i] = h
+        for c in idle:
+            if load[c]:
+                used.add(c)
+                rh_of[c] = (k, load[c])
+    pl = {"ranks": ranks, "cores": cores, "send": send, "relay_of": relay_of, "rh": rh, "rh_of": rh_of}
     _CACHE["p"] = pl
     return pl
 
@@ -116,66 +105,78 @@ def _did(topo, c):
 
 
 def _in_eng(topo, pl, r, k):
-    cs = pl["cores"][pl["stage_of"][r]]
+    cs = pl["cores"]
     for src, ks in pl["send"][r]:
         if k in ks:
             bits = _bits(topo, src, [cs[j] for j in ks])
             return _split(bits, 1)[1], _split(bits, len(ks))[1]
 
 
-def _groups(s):
-    lo, hi, _P, _S, G = STAGES[s]
-    n = hi - lo
-    return [list(range(a, min(a + G, n))) for a in range(0, n, G)]
+def _hand(topo, pl, r):
+    rc = pl["ranks"][r]
+    mine = [k for c, ks in pl["send"][r] if c == rc for k in ks]
+    hel = [(c, ks) for c, ks in pl["send"][r] if c != rc]
+    busy = _bits(topo, rc, [pl["cores"][k] for k in mine]) if mine else []
+    hbits = [b for b in _bits(topo, rc, [c for c, _ks in hel]) if b not in busy] if hel else []
+    return mine, hel, hbits
 
 
-def _ret_masks(topo, pl, s, k, grp):
-    lo = STAGES[s][0]
-    bits = _bits(topo, pl["cores"][s][k], [pl["ranks"][lo + i] for i in grp])
-    return _split(bits, len(grp))
+DIAGS = [[(d - c, c) for c in range(NB) if 0 <= d - c < N] for d in range(N + NB - 1)]
 
 
-def _fwd_masks(topo, pl, s, k):
-    ratio = STAGES[s + 1][2] // STAGES[s][2]
-    src = pl["cores"][s][k]
-    dsts = pl["cores"][s + 1][k * ratio:(k + 1) * ratio]
-    bits = _bits(topo, src, dsts)
-    busy = _bits(topo, src, [c for c in pl["ranks"] if c != src])
-    spare = [b for b in bits if b not in busy]
-    masks, per = _split(spare if len(spare) >= ratio else bits, ratio)
-    return dsts, masks, per
+def _direct(d):
+    return [(i, c) for i, c in DIAGS[d] if i >= ND]
 
 
-def _inflow(g, T, topo, pl, src, r, ks, waits, ls):
-    s = pl["stage_of"][r]
-    lo, _hi, P, _S, _G = STAGES[s]
-    i, w = r - lo, B // P
-    cs = [pl["cores"][s][k] for k in ks]
-    bits = _bits(topo, src, cs)
+def _ret_masks(topo, pl, k, d):
+    bits = _bits(topo, pl["cores"][k], [pl["ranks"][i] for i, _c in _direct(d)])
+    return _split(bits, len(_direct(d)))
+
+
+def _help_masks(topo, pl, k, i):
+    return _split(_bits(topo, pl["rh"][k][i], [pl["ranks"][i]]), NB)
+
+
+def _over_mask(topo, pl, k, i):
+    cc = pl["cores"][k]
+    busy = _bits(topo, cc, pl["ranks"])
+    bits = _bits(topo, cc, [pl["rh"][k][i]])
+    return _split([b for b in bits if b not in busy] or bits, 1)
+
+
+def _ret_eng(topo, pl, k, i, c):
+    return _help_masks(topo, pl, k, i)[1] if i < ND else _ret_masks(topo, pl, k, i + c)[1]
+
+
+def _inflow(g, T, topo, pl, src, r, ks, waits, ls, extra=None):
+    cs = [pl["cores"][k] for k in ks]
+    bits = _bits(topo, src, cs) if cs else []
     for what in ([0, "w", 1, 2] if r == 0 else ["w", 0, 1, 2]):
         g.wait_ge(*waits[what])
-        if what == "w":
+        tr = []
+        if extra is not None:
+            tr, inc = extra(what)
+            ls[0] += inc
+        if cs and what == "w":
             masks, per = _split(bits, 1)
-            tr = [RemoteDMATransfer(dst_ids=[_did(topo, c) for c in cs], dma_engine_mask=masks[0],
-                                    remote_sem=T.sem["w%d" % i], srcs=[T.Wl[:, :]],
-                                    dsts=[T.Wb[:, i * 256:(i + 1) * 256] for _c in cs])]
+            tr = tr + [RemoteDMATransfer(dst_ids=[_did(topo, c) for c in cs], dma_engine_mask=masks[0],
+                                         remote_sem=T.sem["w%d" % r], srcs=[T.Wl[:, :]],
+                                         dsts=[T.Wb[:, r * 256:(r + 1) * 256] for _c in cs])]
             ls[0] += per
-        else:
+        elif cs:
             c = what
             masks, per = _split(bits, len(ks))
-            o = (i * NB + c) * w
-            tr = [RemoteDMATransfer(dst_ids=[_did(topo, cs[j])], dma_engine_mask=masks[j],
-                                    remote_sem=T.sem["x%d_%d" % (i, c)],
-                                    src=T.X[:, c * B + k * w:c * B + (k + 1) * w], dst=T.Xb[:, o:o + w])
-                  for j, k in enumerate(ks)]
+            o = (r * NB + c) * W
+            tr = tr + [RemoteDMATransfer(dst_ids=[_did(topo, cs[j])], dma_engine_mask=masks[j],
+                                         remote_sem=T.sem["x%d_%d" % (r, c)],
+                                         src=T.X[:, c * B + k * W:c * B + (k + 1) * W], dst=T.Xb[:, o:o + W])
+                       for j, k in enumerate(ks)]
             ls[0] += per * len(ks)
         g.remote_dma_fused(tr, local_sem=T.sem.ls)
 
 
 def _rank_prog(g, core, T, topo, pl, r):
     sem = T.sem
-    s = pl["stage_of"][r]
-    lo, _hi, P, _S, _G = STAGES[s]
     ls = [0]
     for c in range(NB):
         g.sync.dma_start(T.X[:, c * B:(c + 1) * B], T.x[:, c * B:(c + 1) * B]).then_inc(sem["xl%d" % c], 16)
@@ -184,24 +185,25 @@ def _rank_prog(g, core, T, topo, pl, r):
     waits = {"w": (sem.wl, 32)}
     for c in range(NB):
         waits[c] = (sem["xl%d" % c], 16)
-    if pl["send"][r][0][0] == core:
-        _inflow(g, T, topo, pl, core, r, pl["send"][r][0][1], waits, ls)
-    else:
-        rel = [c for c, _ks in pl["send"][r]]
-        masks, per = _split(_bits(topo, core, rel), 1)
-        ids = [_did(topo, c) for c in rel]
-        for what in ["w", 0, 1, 2]:
-            g.wait_ge(*waits[what])
-            ap = T.Wl[:, :] if what == "w" else T.X[:, what * B:(what + 1) * B]
-            g.remote_dma_fused([RemoteDMATransfer(dst_ids=ids, dma_engine_mask=masks[0],
-                                                  remote_sem=sem.rw if what == "w" else sem["rx%d" % what],
-                                                  srcs=[ap], dsts=[ap for _c in rel])], local_sem=sem.ls)
-            ls[0] += per
-    i = r - lo
-    grp = [gr for gr in _groups(s) if i in gr][0]
-    total = sum(_ret_masks(topo, pl, s, k, grp)[1] for k in range(P))
+    mine, hel, hbits = _hand(topo, pl, r)
+    hk = [(h, k) for h, ks in hel for k in ks]
+
+    def extra(what):
+        if not hel:
+            return [], 0
+        if what == "w":
+            masks, per = _split(hbits, 1)
+            return [RemoteDMATransfer(dst_ids=[_did(topo, h) for h, _ks in hel], dma_engine_mask=masks[0],
+                                      remote_sem=sem.rw, srcs=[T.Wl[:, :]], dsts=[T.Wl[:, :] for _h in hel])], per
+        masks, per = _split(hbits, len(hk))
+        return [RemoteDMATransfer(dst_ids=[_did(topo, h)], dma_engine_mask=masks[j], remote_sem=sem["rx%d" % what],
+                                  src=T.X[:, what * B + k * W:what * B + (k + 1) * W],
+                                  dst=T.X[:, what * B + k * W:what * B + (k + 1) * W])
+                for j, (h, k) in enumerate(hk)], per * len(hk)
+
+    _inflow(g, T, topo, pl, core, r, mine, waits, ls, extra)
     for c in range(NB):
-        g.sync.wait_ge(sem["y%d" % c], total)
+        g.sync.wait_ge(sem["y%d" % c], sum(_ret_eng(topo, pl, k, r, c) for k in range(P)))
         g.sync.dma_start(T.y[:, c * B:(c + 1) * B], T.YD[:, c * B:(c + 1) * B]).then_inc(sem.st, 16)
     g.sync.wait_ge(sem.st, 16 * NB)
     g.wait_ge(sem.ls, ls[0])
@@ -209,21 +211,18 @@ def _rank_prog(g, core, T, topo, pl, r):
 
 def _relay_prog(g, core, T, topo, pl):
     r, j = pl["relay_of"][core]
-    rel = [c for c, _ks in pl["send"][r]]
-    per = _split(_bits(topo, pl["ranks"][r], rel), 1)[1]
-    waits = {"w": (T.sem.rw, per)}
+    ks = pl["send"][r][j][1]
+    _mine, hel, hbits = _hand(topo, pl, r)
+    waits = {"w": (T.sem.rw, _split(hbits, 1)[1])}
     for c in range(NB):
-        waits[c] = (T.sem["rx%d" % c], per)
+        waits[c] = (T.sem["rx%d" % c], len(ks) * _split(hbits, sum(len(q) for _h, q in hel))[1])
     ls = [0]
-    _inflow(g, T, topo, pl, core, r, pl["send"][r][j][1], waits, ls)
+    _inflow(g, T, topo, pl, core, r, ks, waits, ls)
     g.wait_ge(T.sem.ls, ls[0])
 
 
-def _compute_prog(g, core, T, topo, pl, s, k):
+def _compute_prog(g, core, T, topo, pl, k):
     sem = T.sem
-    lo, hi, P, S, _G = STAGES[s]
-    n, w = hi - lo, B // P
-    wq = w // S
     te, ve = g.tensor, g.vector
     ve.memset(T.zero[:, :], 0.0).then_inc(sem.cz, 1)
     ve.memset(T.idsrc[:, 1:129], 0.0).then_inc(sem.ci, 1)
@@ -235,7 +234,7 @@ def _compute_prog(g, core, T, topo, pl, s, k):
     te.wait_ge(sem.id2, 16)
     ve.wait_ge(sem.cz, 1)
 
-    J = [(c, i, q) for c in range(NB) for i in range(n) for q in range(S)]
+    J = [(i, c) for blocks in DIAGS for i, c in blocks]
     seen = set()
 
     def twait(name, val):
@@ -243,77 +242,81 @@ def _compute_prog(g, core, T, topo, pl, s, k):
             seen.add((name, val))
             te.wait_ge(sem[name], val)
 
-    def off(i, c, q):
-        return (i * NB + c) * w + q * wq
+    def off(i, c):
+        return (i * NB + c) * W
 
     def ps(j):
-        return T["ps%d" % (j % NBANK)][:, 0:wq]
+        return T["ps%d" % (j % NBANK)][:, 0:W]
 
     def pre(j):
-        c, i, q = J[j]
-        crit = lo + i > 0
+        i, c = J[j]
         if j >= NBANK:
-            c0, i0, q0 = J[j - NBANK]
-            twait("v%d_%d" % (c0, q0), i0 + 1)
-        twait("x%d_%d" % (i, c), _in_eng(topo, pl, lo + i, k)[1])
-        o = off(i, c, q)
-        last = te.matmul(ps(j), T.ident[:, :], T.Xb[:, o:o + wq], True, not (crit or c > 0))
+            i0, c0 = J[j - NBANK]
+            twait("v%d" % c0, i0 + 1)
+        twait("x%d_%d" % (i, c), _in_eng(topo, pl, i, k)[1])
+        last = te.matmul(ps(j), T.ident[:, :], T.Xb[:, off(i, c):off(i, c) + W], True, not (i > 0 or c > 0))
         if c > 0:
-            twait("w%d" % i, _in_eng(topo, pl, lo + i, k)[0])
-            twait("v%d_%d" % (c - 1, q), i + 1)
-            o = off(i, c - 1, q)
-            last = te.matmul(ps(j), T.Wb[:, i * 256 + 128:i * 256 + 256], T.Hb[:, o:o + wq], False, not crit)
-        if not crit:
-            last.then_inc(sem["t%d_%d" % (c, q)], 1)
+            twait("w%d" % i, _in_eng(topo, pl, i, k)[0])
+            twait("v%d" % (c - 1), i + 1)
+            o = off(i, c - 1)
+            last = te.matmul(ps(j), T.Wb[:, i * 256 + 128:i * 256 + 256], T.Hb[:, o:o + W], False, not i > 0)
+        if i == 0:
+            last.then_inc(sem["t%d" % c], 1)
 
     def crit(j):
-        c, i, q = J[j]
-        if lo + i == 0:
+        i, c = J[j]
+        if i == 0:
             return
-        twait("w%d" % i, _in_eng(topo, pl, lo + i, k)[0])
-        if i > 0:
-            twait("v%d_%d" % (c, q), i)
-            o = off(i - 1, c, q)
-            rhs = T.Hb[:, o:o + wq]
-        else:
-            ratio = P // STAGES[s - 1][2]
-            twait("h%d" % c, _fwd_masks(topo, pl, s - 1, k // ratio)[2])
-            rhs = T.Hin[:, c * w + q * wq:c * w + (q + 1) * wq]
-        te.matmul(ps(j), T.Wb[:, i * 256:i * 256 + 128], rhs, False, True).then_inc(sem["t%d_%d" % (c, q)], 1)
+        twait("w%d" % i, _in_eng(topo, pl, i, k)[0])
+        twait("v%d" % c, i)
+        o = off(i - 1, c)
+        te.matmul(ps(j), T.Wb[:, i * 256:i * 256 + 128], T.Hb[:, o:o + W], False, True).then_inc(sem["t%d" % c], 1)
 
     pre(0)
     for j in range(len(J)):
         crit(j)
         if j + 1 < len(J):
             pre(j + 1)
-    for j, (c, i, q) in enumerate(J):
-        ve.wait_ge(sem["t%d_%d" % (c, q)], i + 1)
-        o = off(i, c, q)
-        ve.tensor_tensor(T.Hb[:, o:o + wq], ps(j), T.zero[:, 0:wq], AluOpType.max).then_inc(sem["v%d_%d" % (c, q)], 1)
+    for j, (i, c) in enumerate(J):
+        ve.wait_ge(sem["t%d" % c], i + 1)
+        ve.tensor_tensor(T.Hb[:, off(i, c):off(i, c) + W], ps(j), T.zero[:, :], AluOpType.max).then_inc(sem["v%d" % c], 1)
 
     ls = 0
-    for c in range(NB):
-        for grp in _groups(s):
-            for q in range(S):
-                g.wait_ge(sem["v%d_%d" % (c, q)], grp[-1] + 1)
-            if grp[-1] == n - 1 and s + 1 < len(STAGES):
-                dsts, masks, per = _fwd_masks(topo, pl, s, k)
-                w2 = B // STAGES[s + 1][2]
-                o = off(n - 1, c, 0)
-                g.remote_dma_fused([RemoteDMATransfer(dst_ids=[_did(topo, d)], dma_engine_mask=masks[jj],
-                                                      remote_sem=sem["h%d" % c],
-                                                      src=T.Hb[:, o + jj * w2:o + (jj + 1) * w2],
-                                                      dst=T.Hin[:, c * w2:(c + 1) * w2])
-                                    for jj, d in enumerate(dsts)], local_sem=sem.ls)
-                ls += per * len(dsts)
-            masks, per = _ret_masks(topo, pl, s, k, grp)
-            g.remote_dma_fused([RemoteDMATransfer(dst_ids=[_did(topo, pl["ranks"][lo + i])],
+    for d, blocks in enumerate(DIAGS):
+        for i, c in blocks:
+            g.wait_ge(sem["v%d" % c], i + 1)
+        i = d - (NB - 1)
+        if 0 <= i < ND:
+            masks, per = _over_mask(topo, pl, k, i)
+            g.remote_dma_fused([RemoteDMATransfer(dst_ids=[_did(topo, pl["rh"][k][i])], dma_engine_mask=masks[0],
+                                                  remote_sem=sem["g%d" % i],
+                                                  src=T.Hb[:, off(i, 0):off(i, 0) + NB * W],
+                                                  dst=T.Hb[:, off(i, 0):off(i, 0) + NB * W])], local_sem=sem.ls)
+            ls += per
+        if _direct(d):
+            masks, per = _ret_masks(topo, pl, k, d)
+            g.remote_dma_fused([RemoteDMATransfer(dst_ids=[_did(topo, pl["ranks"][i])],
                                                   dma_engine_mask=masks[jj], remote_sem=sem["y%d" % c],
-                                                  src=T.Hb[:, off(i, c, 0):off(i, c, 0) + w],
-                                                  dst=T.YD[:, c * B + k * w:c * B + (k + 1) * w])
-                                for jj, i in enumerate(grp)], local_sem=sem.ls)
-            ls += per * len(grp)
+                                                  src=T.Hb[:, off(i, c):off(i, c) + W],
+                                                  dst=T.YD[:, c * B + k * W:c * B + (k + 1) * W])
+                                for jj, (i, c) in enumerate(_direct(d))], local_sem=sem.ls)
+            ls += per * len(_direct(d))
     g.wait_ge(sem.ls, ls)
+
+
+def _scatter_prog(g, core, T, topo, pl):
+    k, mine = pl["rh_of"][core]
+    ls = 0
+    for i in mine:
+        g.wait_ge(T.sem["g%d" % i], _over_mask(topo, pl, k, i)[1])
+        masks, per = _help_masks(topo, pl, k, i)
+        o = i * NB * W
+        g.remote_dma_fused([RemoteDMATransfer(dst_ids=[_did(topo, pl["ranks"][i])], dma_engine_mask=masks[c],
+                                              remote_sem=T.sem["y%d" % c], src=T.Hb[:, o + c * W:o + (c + 1) * W],
+                                              dst=T.YD[:, c * B + k * W:c * B + (k + 1) * W])
+                            for c in range(NB)], local_sem=T.sem.ls)
+        ls += per * NB
+    g.wait_ge(T.sem.ls, ls)
 
 
 def rank_program(g, core, T, topo):
@@ -321,11 +324,9 @@ def rank_program(g, core, T, topo):
     rank = T.rank_of(core)
     if rank is not None:
         _rank_prog(g, core, T, topo, pl, rank)
-        return
-    if core in pl["relay_of"]:
+    elif core in pl["relay_of"]:
         _relay_prog(g, core, T, topo, pl)
-        return
-    for s, cs in enumerate(pl["cores"]):
-        if core in cs:
-            _compute_prog(g, core, T, topo, pl, s, cs.index(core))
-            return
+    elif core in pl["rh_of"]:
+        _scatter_prog(g, core, T, topo, pl)
+    elif core in pl["cores"]:
+        _compute_prog(g, core, T, topo, pl, pl["cores"].index(core))

@@ -24,8 +24,8 @@ SCRATCH = {
 for _b in range(NBANK):
     SCRATCH["ps%d" % _b] = ("psum", [128, 512], "float32")
 
-SEMAPHORES = (["wl", "st", "ls", "rw", "cz", "ci", "id1", "id2"]
-              + ["%s%d" % (a, c) for a in ("xl", "rx", "y", "t", "v") for c in range(NB)]
+SEMAPHORES = (["wl", "st", "ls", "rw", "rx0", "cz", "ci", "id1", "id2"]
+              + ["%s%d" % (a, c) for a in ("xl", "y", "t", "v") for c in range(NB)]
               + ["w%d" % i for i in range(N)] + ["g%d" % i for i in range(N)]
               + ["x%d_%d" % (i, c) for i in range(N) for c in range(NB)])
 
@@ -56,33 +56,45 @@ def _plan(T, topo):
     chips = sorted(set(topo.chip(c) for c in allc))
     on = {ch: [c for c in allc if topo.chip(c) == ch] for ch in chips}
     dies = sorted(set(topo.die(c) for c in allc))
-    cores = []
-    for ch in sorted(chips, key=lambda ch: (sum(1 for c in on[ch] if c in ranks), ch)):
-        if len(cores) == P:
-            break
-        want = dies[len(cores) % len(dies)]
-        cand = [c for c in on[ch] if c in free and c not in used]
-        cand.sort(key=lambda c: (topo.die(c) != want, c))
-        if cand:
+    planes = []
+    for ch in chips:
+        for p in planes:
+            if topo.same_plane(p[0], ch):
+                p.append(ch)
+                break
+        else:
+            planes.append([ch])
+    here = {ch: [r for r, c in enumerate(ranks) if topo.chip(c) == ch] for ch in chips}
+    near = {ch: [r for o in chips if o == ch or topo.mates(o, ch) for r in here[o]] for ch in chips}
+    cores, groups = [], []
+    for p in planes:
+        groups.append([])
+        for ch in sorted(p, key=lambda ch: (not near[ch], len(here[ch]), -min(here[ch] + [len(ranks)]), ch))[:P // len(planes)]:
+            want = dies[len(cores) % len(dies)]
+            cand = [c for c in on[ch] if c in free and c not in used]
+            cand.sort(key=lambda c: (sum(1 for x in on[ch] if x in ranks and x not in free and topo.die(x) == topo.die(c)),
+                                     topo.die(c) != want, c))
+            groups[-1].append(len(cores))
             cores.append(cand[0])
             used.add(cand[0])
     send, relay_of = {}, {}
     for r, rc in enumerate(ranks):
-        hel = [c for c in on[topo.chip(rc)] if c not in used and topo.die(c) == topo.die(rc)]
-        hel.sort(key=lambda c: (-sum(1 for x in cores if topo.may_write(c, x)), c))
-        snd = [rc] + hel[:NREL]
-        load = {c: [] for c in snd}
-        for k in sorted(range(P), key=lambda k: (sum(1 for c in snd if topo.may_write(c, cores[k])), k)):
-            cand = [c for c in snd if topo.may_write(c, cores[k])]
-            load[min(cand, key=lambda c: (len(load[c]), snd.index(c)))].append(k)
-        send[r] = [(c, sorted(load[c])) for c in snd if load[c]]
+        idle = [c for c in on[topo.chip(rc)] if c not in used and topo.die(c) == topo.die(rc)]
+        for grp in groups:
+            rest = [k for k in range(P) if k not in grp]
+            hel = [c for c in idle if all(topo.may_write(c, cores[k]) for k in rest)]
+            hel.sort(key=lambda c: (sum(1 for x in cores if topo.may_write(c, x)), c))
+            if all(topo.may_write(rc, cores[k]) for k in grp) and len(hel) >= NREL:
+                n = len(rest) // NREL
+                send[r] = [(rc, list(grp))] + [(hel[j], rest[j * n:(j + 1) * n]) for j in range(NREL)]
+                break
         for j, (c, _ks) in enumerate(send[r]):
             if c != rc:
                 used.add(c)
                 relay_of[c] = (r, j)
     rh, rh_of = [], {}
     for k, cc in enumerate(cores):
-        idle = [c for c in on[topo.chip(cc)] if c not in used]
+        idle = [c for c in on[topo.chip(cc)] if c not in ranks and c not in cores]
         load = {c: [] for c in idle}
         rh.append({})
         for i in range(ND):
@@ -92,7 +104,6 @@ def _plan(T, topo):
             rh[k][i] = h
         for c in idle:
             if load[c]:
-                used.add(c)
                 rh_of[c] = (k, load[c])
     pl = {"ranks": ranks, "cores": cores, "send": send, "relay_of": relay_of, "rh": rh, "rh_of": rh_of}
     _CACHE["p"] = pl
@@ -104,20 +115,24 @@ def _did(topo, c):
     return DstId(rid=rid, pnc=pid)
 
 
-def _in_eng(topo, pl, r, k):
+XCALLS = [[0, 1], [2]]
+
+
+def _in_eng(topo, pl, r, k, c):
     cs = pl["cores"]
+    grp = [q for q in XCALLS if c in q][0]
     for src, ks in pl["send"][r]:
         if k in ks:
             bits = _bits(topo, src, [cs[j] for j in ks])
-            return _split(bits, 1)[1], _split(bits, len(ks))[1]
+            return _split(bits, 1)[1], _split(bits, len(ks) * len(grp))[1]
 
 
 def _hand(topo, pl, r):
     rc = pl["ranks"][r]
     mine = [k for c, ks in pl["send"][r] if c == rc for k in ks]
     hel = [(c, ks) for c, ks in pl["send"][r] if c != rc]
-    busy = _bits(topo, rc, [pl["cores"][k] for k in mine]) if mine else []
-    hbits = [b for b in _bits(topo, rc, [c for c, _ks in hel]) if b not in busy] if hel else []
+    busy = _bits(topo, rc, [pl["cores"][k] for k in mine])
+    hbits = [b for b in _bits(topo, rc, [c for c, _ks in hel]) if b not in busy]
     return mine, hel, hbits
 
 
@@ -148,76 +163,79 @@ def _ret_eng(topo, pl, k, i, c):
     return _help_masks(topo, pl, k, i)[1] if i < ND else _ret_masks(topo, pl, k, i + c)[1]
 
 
-def _inflow(g, T, topo, pl, src, r, ks, waits, ls, extra=None):
+def _wlo(r):
+    return 128 if r == 0 else 0
+
+
+def _send_w(T, topo, pl, src, r, ks):
     cs = [pl["cores"][k] for k in ks]
-    bits = _bits(topo, src, cs) if cs else []
-    for what in ([0, "w", 1, 2] if r == 0 else ["w", 0, 1, 2]):
-        g.wait_ge(*waits[what])
-        tr = []
-        if extra is not None:
-            tr, inc = extra(what)
-            ls[0] += inc
-        if cs and what == "w":
-            masks, per = _split(bits, 1)
-            tr = tr + [RemoteDMATransfer(dst_ids=[_did(topo, c) for c in cs], dma_engine_mask=masks[0],
-                                         remote_sem=T.sem["w%d" % r], srcs=[T.Wl[:, :]],
-                                         dsts=[T.Wb[:, r * 256:(r + 1) * 256] for _c in cs])]
-            ls[0] += per
-        elif cs:
-            c = what
-            masks, per = _split(bits, len(ks))
-            o = (r * NB + c) * W
-            tr = tr + [RemoteDMATransfer(dst_ids=[_did(topo, cs[j])], dma_engine_mask=masks[j],
-                                         remote_sem=T.sem["x%d_%d" % (r, c)],
-                                         src=T.X[:, c * B + k * W:c * B + (k + 1) * W], dst=T.Xb[:, o:o + W])
-                       for j, k in enumerate(ks)]
-            ls[0] += per * len(ks)
-        g.remote_dma_fused(tr, local_sem=T.sem.ls)
+    masks, per = _split(_bits(topo, src, cs), 1)
+    return [RemoteDMATransfer(dst_ids=[_did(topo, c) for c in cs], dma_engine_mask=masks[0], remote_sem=T.sem["w%d" % r],
+                              srcs=[T.Wl[:, _wlo(r):256]],
+                              dsts=[T.Wb[:, r * 256 + _wlo(r):(r + 1) * 256] for _c in cs])], per
+
+
+def _send_x(T, topo, pl, src, r, ks, grp):
+    what = [(c, k) for c in grp for k in ks]
+    masks, per = _split(_bits(topo, src, [pl["cores"][k] for k in ks]), len(what))
+    return [RemoteDMATransfer(dst_ids=[_did(topo, pl["cores"][k])], dma_engine_mask=masks[j],
+                              remote_sem=T.sem["x%d_%d" % (r, c)], src=T.X[:, c * B + k * W:c * B + (k + 1) * W],
+                              dst=T.Xb[:, (r * NB + c) * W:(r * NB + c + 1) * W])
+            for j, (c, k) in enumerate(what)], per * len(what)
 
 
 def _rank_prog(g, core, T, topo, pl, r):
     sem = T.sem
-    ls = [0]
+    ls = 0
     for c in range(NB):
         g.sync.dma_start(T.X[:, c * B:(c + 1) * B], T.x[:, c * B:(c + 1) * B]).then_inc(sem["xl%d" % c], 16)
-    g.scalar.dma_start(T.Wl[:, 0:128], T.wv[:, :]).then_inc(sem.wl, 16)
+    nw = 0
+    if r > 0:
+        g.scalar.dma_start(T.Wl[:, 0:128], T.wv[:, :]).then_inc(sem.wl, 16)
+        nw += 16
     g.scalar.dma_start(T.Wl[:, 128:256], T.wh[:, :]).then_inc(sem.wl, 16)
-    waits = {"w": (sem.wl, 32)}
-    for c in range(NB):
-        waits[c] = (sem["xl%d" % c], 16)
+    nw += 16
     mine, hel, hbits = _hand(topo, pl, r)
-    hk = [(h, k) for h, ks in hel for k in ks]
-
-    def extra(what):
-        if not hel:
-            return [], 0
-        if what == "w":
-            masks, per = _split(hbits, 1)
-            return [RemoteDMATransfer(dst_ids=[_did(topo, h) for h, _ks in hel], dma_engine_mask=masks[0],
-                                      remote_sem=sem.rw, srcs=[T.Wl[:, :]], dsts=[T.Wl[:, :] for _h in hel])], per
-        masks, per = _split(hbits, len(hk))
-        return [RemoteDMATransfer(dst_ids=[_did(topo, h)], dma_engine_mask=masks[j], remote_sem=sem["rx%d" % what],
-                                  src=T.X[:, what * B + k * W:what * B + (k + 1) * W],
-                                  dst=T.X[:, what * B + k * W:what * B + (k + 1) * W])
-                for j, (h, k) in enumerate(hk)], per * len(hk)
-
-    _inflow(g, T, topo, pl, core, r, mine, waits, ls, extra)
+    g.wait_ge(sem.wl, nw)
+    masks, per = _split(hbits, 1)
+    tr, inc = _send_w(T, topo, pl, core, r, mine)
+    g.remote_dma_fused([RemoteDMATransfer(dst_ids=[_did(topo, h) for h, _ks in hel], dma_engine_mask=masks[0],
+                                          remote_sem=sem.rw, srcs=[T.Wl[:, _wlo(r):256]],
+                                          dsts=[T.Wl[:, _wlo(r):256] for _h in hel])] + tr, local_sem=sem.ls)
+    ls += per + inc
+    for c in range(NB):
+        g.wait_ge(sem["xl%d" % c], 16)
+    what = [(c, h, ks) for c in range(NB) for h, ks in hel]
+    masks, per = _split(hbits, len(what))
+    g.remote_dma_fused([RemoteDMATransfer(dst_ids=[_did(topo, h)], dma_engine_mask=masks[j], remote_sem=sem.rx0,
+                                          src=T.X[:, c * B + ks[0] * W:c * B + (ks[-1] + 1) * W],
+                                          dst=T.X[:, c * B + ks[0] * W:c * B + (ks[-1] + 1) * W])
+                        for j, (c, h, ks) in enumerate(what)], local_sem=sem.ls)
+    ls += per * len(what)
+    for grp in XCALLS:
+        tr, inc = _send_x(T, topo, pl, core, r, mine, grp)
+        g.remote_dma_fused(tr, local_sem=sem.ls)
+        ls += inc
     for c in range(NB):
         g.sync.wait_ge(sem["y%d" % c], sum(_ret_eng(topo, pl, k, r, c) for k in range(P)))
         g.sync.dma_start(T.y[:, c * B:(c + 1) * B], T.YD[:, c * B:(c + 1) * B]).then_inc(sem.st, 16)
     g.sync.wait_ge(sem.st, 16 * NB)
-    g.wait_ge(sem.ls, ls[0])
+    g.wait_ge(sem.ls, ls)
 
 
-def _relay_prog(g, core, T, topo, pl):
+def _relay_prog(g, core, T, topo, pl, ls):
     r, j = pl["relay_of"][core]
     ks = pl["send"][r][j][1]
     _mine, hel, hbits = _hand(topo, pl, r)
-    waits = {"w": (T.sem.rw, _split(hbits, 1)[1])}
-    for c in range(NB):
-        waits[c] = (T.sem["rx%d" % c], len(ks) * _split(hbits, sum(len(q) for _h, q in hel))[1])
-    ls = [0]
-    _inflow(g, T, topo, pl, core, r, ks, waits, ls)
+    g.wait_ge(T.sem.rw, _split(hbits, 1)[1])
+    tr, inc = _send_w(T, topo, pl, core, r, ks)
+    g.remote_dma_fused(tr, local_sem=T.sem.ls)
+    ls[0] += inc
+    g.wait_ge(T.sem.rx0, NB * _split(hbits, NB * len(hel))[1])
+    for grp in XCALLS:
+        tr, inc = _send_x(T, topo, pl, core, r, ks, grp)
+        g.remote_dma_fused(tr, local_sem=T.sem.ls)
+        ls[0] += inc
     g.wait_ge(T.sem.ls, ls[0])
 
 
@@ -253,10 +271,10 @@ def _compute_prog(g, core, T, topo, pl, k):
         if j >= NBANK:
             i0, c0 = J[j - NBANK]
             twait("v%d" % c0, i0 + 1)
-        twait("x%d_%d" % (i, c), _in_eng(topo, pl, i, k)[1])
+        twait("x%d_%d" % (i, c), _in_eng(topo, pl, i, k, c)[1])
         last = te.matmul(ps(j), T.ident[:, :], T.Xb[:, off(i, c):off(i, c) + W], True, not (i > 0 or c > 0))
         if c > 0:
-            twait("w%d" % i, _in_eng(topo, pl, i, k)[0])
+            twait("w%d" % i, _in_eng(topo, pl, i, k, c)[0])
             twait("v%d" % (c - 1), i + 1)
             o = off(i, c - 1)
             last = te.matmul(ps(j), T.Wb[:, i * 256 + 128:i * 256 + 256], T.Hb[:, o:o + W], False, not i > 0)
@@ -267,7 +285,7 @@ def _compute_prog(g, core, T, topo, pl, k):
         i, c = J[j]
         if i == 0:
             return
-        twait("w%d" % i, _in_eng(topo, pl, i, k)[0])
+        twait("w%d" % i, _in_eng(topo, pl, i, k, c)[0])
         twait("v%d" % c, i)
         o = off(i - 1, c)
         te.matmul(ps(j), T.Wb[:, i * 256:i * 256 + 128], T.Hb[:, o:o + W], False, True).then_inc(sem["t%d" % c], 1)
@@ -304,9 +322,8 @@ def _compute_prog(g, core, T, topo, pl, k):
     g.wait_ge(sem.ls, ls)
 
 
-def _scatter_prog(g, core, T, topo, pl):
+def _scatter_prog(g, core, T, topo, pl, ls):
     k, mine = pl["rh_of"][core]
-    ls = 0
     for i in mine:
         g.wait_ge(T.sem["g%d" % i], _over_mask(topo, pl, k, i)[1])
         masks, per = _help_masks(topo, pl, k, i)
@@ -315,8 +332,8 @@ def _scatter_prog(g, core, T, topo, pl):
                                               remote_sem=T.sem["y%d" % c], src=T.Hb[:, o + c * W:o + (c + 1) * W],
                                               dst=T.YD[:, c * B + k * W:c * B + (k + 1) * W])
                             for c in range(NB)], local_sem=T.sem.ls)
-        ls += per * NB
-    g.wait_ge(T.sem.ls, ls)
+        ls[0] += per * NB
+    g.wait_ge(T.sem.ls, ls[0])
 
 
 def rank_program(g, core, T, topo):
@@ -324,9 +341,11 @@ def rank_program(g, core, T, topo):
     rank = T.rank_of(core)
     if rank is not None:
         _rank_prog(g, core, T, topo, pl, rank)
-    elif core in pl["relay_of"]:
-        _relay_prog(g, core, T, topo, pl)
-    elif core in pl["rh_of"]:
-        _scatter_prog(g, core, T, topo, pl)
     elif core in pl["cores"]:
         _compute_prog(g, core, T, topo, pl, pl["cores"].index(core))
+    else:
+        ls = [0]
+        if core in pl["relay_of"]:
+            _relay_prog(g, core, T, topo, pl, ls)
+        if core in pl["rh_of"]:
+            _scatter_prog(g, core, T, topo, pl, ls)

from concourse.bass import DstId, RemoteDMATransfer
from concourse.mybir import AluOpType

NB, B = 3, 512
N = 16
P = 8
W = B // P
NREL = 2
NBANK = 8
ND = N - 2

SCRATCH = {
    "Wl": ("sbuf", [128, 256], "bfloat16"),
    "X": ("sbuf", [128, NB * B], "bfloat16"),
    "YD": ("sbuf", [128, NB * B], "bfloat16"),
    "Wb": ("sbuf", [128, N * 256], "bfloat16"),
    "Xb": ("sbuf", [128, N * NB * W], "bfloat16"),
    "Hb": ("sbuf", [128, N * NB * W], "bfloat16"),
    "idsrc": ("sbuf", [128, 129], "bfloat16"),
    "idd": ("dram", [129, 128], "bfloat16"),
    "ident": ("sbuf", [128, 128], "bfloat16"),
    "zero": ("sbuf", [128, W], "float32"),
}
for _b in range(NBANK):
    SCRATCH["ps%d" % _b] = ("psum", [128, 512], "float32")

SEMAPHORES = (["wl", "st", "ls", "rw", "rx0", "cz", "ci", "id1", "id2"]
              + ["%s%d" % (a, c) for a in ("xl", "y", "t", "v") for c in range(NB)]
              + ["w%d" % i for i in range(N)] + ["g%d" % i for i in range(N)]
              + ["x%d_%d" % (i, c) for i in range(N) for c in range(NB)])

_CACHE = {}


def _bits(topo, src, dsts):
    m = -1
    for d in dsts:
        m &= topo.mask(src, d)
    return [b for b in range(64) if (m >> b) & 1]


def _split(bits, m):
    per = 1
    while per * 2 * m <= len(bits):
        per *= 2
    return [sum(1 << b for b in bits[j * per:(j + 1) * per]) for j in range(m)], per


def _plan(T, topo):
    if "p" in _CACHE:
        return _CACHE["p"]
    allc = list(range(topo.CHIPS * topo.CORES_PER_CHIP))
    ranks = list(T.cores)
    used = set(ranks)
    free = [c for c in allc if all(topo.may_write(c, d) for d in allc if d != c)]
    chips = sorted(set(topo.chip(c) for c in allc))
    on = {ch: [c for c in allc if topo.chip(c) == ch] for ch in chips}
    dies = sorted(set(topo.die(c) for c in allc))
    planes = []
    for ch in chips:
        for p in planes:
            if topo.same_plane(p[0], ch):
                p.append(ch)
                break
        else:
            planes.append([ch])
    here = {ch: [r for r, c in enumerate(ranks) if topo.chip(c) == ch] for ch in chips}
    near = {ch: [r for o in chips if o == ch or topo.mates(o, ch) for r in here[o]] for ch in chips}
    cores, groups = [], []
    for p in planes:
        groups.append([])
        for ch in sorted(p, key=lambda ch: (not near[ch], len(here[ch]), -min(here[ch] + [len(ranks)]), ch))[:P // len(planes)]:
            want = dies[len(cores) % len(dies)]
            cand = [c for c in on[ch] if c in free and c not in used]
            cand.sort(key=lambda c: (sum(1 for x in on[ch] if x in ranks and x not in free and topo.die(x) == topo.die(c)),
                                     topo.die(c) != want, c))
            groups[-1].append(len(cores))
            cores.append(cand[0])
            used.add(cand[0])
    send, relay_of = {}, {}
    for r, rc in enumerate(ranks):
        idle = [c for c in on[topo.chip(rc)] if c not in used and topo.die(c) == topo.die(rc)]
        for grp in groups:
            rest = [k for k in range(P) if k not in grp]
            hel = [c for c in idle if all(topo.may_write(c, cores[k]) for k in rest)]
            hel.sort(key=lambda c: (sum(1 for x in cores if topo.may_write(c, x)), c))
            if all(topo.may_write(rc, cores[k]) for k in grp) and len(hel) >= NREL:
                n = len(rest) // NREL
                send[r] = [(rc, list(grp))] + [(hel[j], rest[j * n:(j + 1) * n]) for j in range(NREL)]
                break
        for j, (c, _ks) in enumerate(send[r]):
            if c != rc:
                used.add(c)
                relay_of[c] = (r, j)
    rh, rh_of = [], {}
    for k, cc in enumerate(cores):
        idle = [c for c in on[topo.chip(cc)] if c not in ranks and c not in cores]
        load = {c: [] for c in idle}
        rh.append({})
        for i in range(ND):
            cand = [c for c in idle if topo.may_write(c, ranks[i])]
            h = min(cand, key=lambda c: (len(load[c]), sum(1 for x in ranks if topo.may_write(c, x)), c))
            load[h].append(i)
            rh[k][i] = h
        for c in idle:
            if load[c]:
                rh_of[c] = (k, load[c])
    pl = {"ranks": ranks, "cores": cores, "send": send, "relay_of": relay_of, "rh": rh, "rh_of": rh_of}
    _CACHE["p"] = pl
    return pl


def _did(topo, c):
    rid, pid, _se = topo.addr(c)
    return DstId(rid=rid, pnc=pid)


XCALLS = [[0, 1], [2]]


def _in_eng(topo, pl, r, k, c):
    cs = pl["cores"]
    grp = [q for q in XCALLS if c in q][0]
    for src, ks in pl["send"][r]:
        if k in ks:
            bits = _bits(topo, src, [cs[j] for j in ks])
            return _split(bits, 1)[1], _split(bits, len(ks) * len(grp))[1]


def _hand(topo, pl, r):
    rc = pl["ranks"][r]
    mine = [k for c, ks in pl["send"][r] if c == rc for k in ks]
    hel = [(c, ks) for c, ks in pl["send"][r] if c != rc]
    busy = _bits(topo, rc, [pl["cores"][k] for k in mine])
    hbits = [b for b in _bits(topo, rc, [c for c, _ks in hel]) if b not in busy]
    return mine, hel, hbits


DIAGS = [[(d - c, c) for c in range(NB) if 0 <= d - c < N] for d in range(N + NB - 1)]


def _direct(d):
    return [(i, c) for i, c in DIAGS[d] if i >= ND]


def _ret_masks(topo, pl, k, d):
    bits = _bits(topo, pl["cores"][k], [pl["ranks"][i] for i, _c in _direct(d)])
    return _split(bits, len(_direct(d)))


def _help_masks(topo, pl, k, i):
    return _split(_bits(topo, pl["rh"][k][i], [pl["ranks"][i]]), NB)


def _over_mask(topo, pl, k, i):
    cc = pl["cores"][k]
    busy = _bits(topo, cc, pl["ranks"])
    bits = _bits(topo, cc, [pl["rh"][k][i]])
    return _split([b for b in bits if b not in busy] or bits, 1)


def _ret_eng(topo, pl, k, i, c):
    return _help_masks(topo, pl, k, i)[1] if i < ND else _ret_masks(topo, pl, k, i + c)[1]


def _wlo(r):
    return 128 if r == 0 else 0


def _send_w(T, topo, pl, src, r, ks):
    cs = [pl["cores"][k] for k in ks]
    masks, per = _split(_bits(topo, src, cs), 1)
    return [RemoteDMATransfer(dst_ids=[_did(topo, c) for c in cs], dma_engine_mask=masks[0], remote_sem=T.sem["w%d" % r],
                              srcs=[T.Wl[:, _wlo(r):256]],
                              dsts=[T.Wb[:, r * 256 + _wlo(r):(r + 1) * 256] for _c in cs])], per


def _send_x(T, topo, pl, src, r, ks, grp):
    what = [(c, k) for c in grp for k in ks]
    masks, per = _split(_bits(topo, src, [pl["cores"][k] for k in ks]), len(what))
    return [RemoteDMATransfer(dst_ids=[_did(topo, pl["cores"][k])], dma_engine_mask=masks[j],
                              remote_sem=T.sem["x%d_%d" % (r, c)], src=T.X[:, c * B + k * W:c * B + (k + 1) * W],
                              dst=T.Xb[:, (r * NB + c) * W:(r * NB + c + 1) * W])
            for j, (c, k) in enumerate(what)], per * len(what)


def _rank_prog(g, core, T, topo, pl, r):
    sem = T.sem
    ls = 0
    for c in range(NB):
        g.sync.dma_start(T.X[:, c * B:(c + 1) * B], T.x[:, c * B:(c + 1) * B]).then_inc(sem["xl%d" % c], 16)
    nw = 0
    if r > 0:
        g.scalar.dma_start(T.Wl[:, 0:128], T.wv[:, :]).then_inc(sem.wl, 16)
        nw += 16
    g.scalar.dma_start(T.Wl[:, 128:256], T.wh[:, :]).then_inc(sem.wl, 16)
    nw += 16
    mine, hel, hbits = _hand(topo, pl, r)
    g.wait_ge(sem.wl, nw)
    masks, per = _split(hbits, 1)
    tr, inc = _send_w(T, topo, pl, core, r, mine)
    g.remote_dma_fused([RemoteDMATransfer(dst_ids=[_did(topo, h) for h, _ks in hel], dma_engine_mask=masks[0],
                                          remote_sem=sem.rw, srcs=[T.Wl[:, _wlo(r):256]],
                                          dsts=[T.Wl[:, _wlo(r):256] for _h in hel])] + tr, local_sem=sem.ls)
    ls += per + inc
    for c in range(NB):
        g.wait_ge(sem["xl%d" % c], 16)
    what = [(c, h, ks) for c in range(NB) for h, ks in hel]
    masks, per = _split(hbits, len(what))
    g.remote_dma_fused([RemoteDMATransfer(dst_ids=[_did(topo, h)], dma_engine_mask=masks[j], remote_sem=sem.rx0,
                                          src=T.X[:, c * B + ks[0] * W:c * B + (ks[-1] + 1) * W],
                                          dst=T.X[:, c * B + ks[0] * W:c * B + (ks[-1] + 1) * W])
                        for j, (c, h, ks) in enumerate(what)], local_sem=sem.ls)
    ls += per * len(what)
    for grp in XCALLS:
        tr, inc = _send_x(T, topo, pl, core, r, mine, grp)
        g.remote_dma_fused(tr, local_sem=sem.ls)
        ls += inc
    for c in range(NB):
        g.sync.wait_ge(sem["y%d" % c], sum(_ret_eng(topo, pl, k, r, c) for k in range(P)))
        g.sync.dma_start(T.y[:, c * B:(c + 1) * B], T.YD[:, c * B:(c + 1) * B]).then_inc(sem.st, 16)
    g.sync.wait_ge(sem.st, 16 * NB)
    g.wait_ge(sem.ls, ls)


def _relay_prog(g, core, T, topo, pl, ls):
    r, j = pl["relay_of"][core]
    ks = pl["send"][r][j][1]
    _mine, hel, hbits = _hand(topo, pl, r)
    g.wait_ge(T.sem.rw, _split(hbits, 1)[1])
    tr, inc = _send_w(T, topo, pl, core, r, ks)
    g.remote_dma_fused(tr, local_sem=T.sem.ls)
    ls[0] += inc
    g.wait_ge(T.sem.rx0, NB * _split(hbits, NB * len(hel))[1])
    for grp in XCALLS:
        tr, inc = _send_x(T, topo, pl, core, r, ks, grp)
        g.remote_dma_fused(tr, local_sem=T.sem.ls)
        ls[0] += inc
    g.wait_ge(T.sem.ls, ls[0])


def _compute_prog(g, core, T, topo, pl, k):
    sem = T.sem
    te, ve = g.tensor, g.vector
    ve.memset(T.zero[:, :], 0.0).then_inc(sem.cz, 1)
    ve.memset(T.idsrc[:, 1:129], 0.0).then_inc(sem.ci, 1)
    ve.memset(T.idsrc[:, 0:1], 1.0).then_inc(sem.ci, 1)
    g.sync.wait_ge(sem.ci, 2)
    g.sync.dma_start(T.idd[:, :], T.idsrc[:, :]).then_inc(sem.id1, 16)
    g.sync.wait_ge(sem.id1, 16)
    g.sync.dma_start(T.ident[:, :], T.idd[0:128, :]).then_inc(sem.id2, 16)
    te.wait_ge(sem.id2, 16)
    ve.wait_ge(sem.cz, 1)

    J = [(i, c) for blocks in DIAGS for i, c in blocks]
    seen = set()

    def twait(name, val):
        if (name, val) not in seen:
            seen.add((name, val))
            te.wait_ge(sem[name], val)

    def off(i, c):
        return (i * NB + c) * W

    def ps(j):
        return T["ps%d" % (j % NBANK)][:, 0:W]

    def pre(j):
        i, c = J[j]
        if j >= NBANK:
            i0, c0 = J[j - NBANK]
            twait("v%d" % c0, i0 + 1)
        twait("x%d_%d" % (i, c), _in_eng(topo, pl, i, k, c)[1])
        last = te.matmul(ps(j), T.ident[:, :], T.Xb[:, off(i, c):off(i, c) + W], True, not (i > 0 or c > 0))
        if c > 0:
            twait("w%d" % i, _in_eng(topo, pl, i, k, c)[0])
            twait("v%d" % (c - 1), i + 1)
            o = off(i, c - 1)
            last = te.matmul(ps(j), T.Wb[:, i * 256 + 128:i * 256 + 256], T.Hb[:, o:o + W], False, not i > 0)
        if i == 0:
            last.then_inc(sem["t%d" % c], 1)

    def crit(j):
        i, c = J[j]
        if i == 0:
            return
        twait("w%d" % i, _in_eng(topo, pl, i, k, c)[0])
        twait("v%d" % c, i)
        o = off(i - 1, c)
        te.matmul(ps(j), T.Wb[:, i * 256:i * 256 + 128], T.Hb[:, o:o + W], False, True).then_inc(sem["t%d" % c], 1)

    pre(0)
    for j in range(len(J)):
        crit(j)
        if j + 1 < len(J):
            pre(j + 1)
    for j, (i, c) in enumerate(J):
        ve.wait_ge(sem["t%d" % c], i + 1)
        ve.tensor_tensor(T.Hb[:, off(i, c):off(i, c) + W], ps(j), T.zero[:, :], AluOpType.max).then_inc(sem["v%d" % c], 1)

    ls = 0
    for d, blocks in enumerate(DIAGS):
        for i, c in blocks:
            g.wait_ge(sem["v%d" % c], i + 1)
        i = d - (NB - 1)
        if 0 <= i < ND:
            masks, per = _over_mask(topo, pl, k, i)
            g.remote_dma_fused([RemoteDMATransfer(dst_ids=[_did(topo, pl["rh"][k][i])], dma_engine_mask=masks[0],
                                                  remote_sem=sem["g%d" % i],
                                                  src=T.Hb[:, off(i, 0):off(i, 0) + NB * W],
                                                  dst=T.Hb[:, off(i, 0):off(i, 0) + NB * W])], local_sem=sem.ls)
            ls += per
        if _direct(d):
            masks, per = _ret_masks(topo, pl, k, d)
            g.remote_dma_fused([RemoteDMATransfer(dst_ids=[_did(topo, pl["ranks"][i])],
                                                  dma_engine_mask=masks[jj], remote_sem=sem["y%d" % c],
                                                  src=T.Hb[:, off(i, c):off(i, c) + W],
                                                  dst=T.YD[:, c * B + k * W:c * B + (k + 1) * W])
                                for jj, (i, c) in enumerate(_direct(d))], local_sem=sem.ls)
            ls += per * len(_direct(d))
    g.wait_ge(sem.ls, ls)


def _scatter_prog(g, core, T, topo, pl, ls):
    k, mine = pl["rh_of"][core]
    for i in mine:
        g.wait_ge(T.sem["g%d" % i], _over_mask(topo, pl, k, i)[1])
        masks, per = _help_masks(topo, pl, k, i)
        o = i * NB * W
        g.remote_dma_fused([RemoteDMATransfer(dst_ids=[_did(topo, pl["ranks"][i])], dma_engine_mask=masks[c],
                                              remote_sem=T.sem["y%d" % c], src=T.Hb[:, o + c * W:o + (c + 1) * W],
                                              dst=T.YD[:, c * B + k * W:c * B + (k + 1) * W])
                            for c in range(NB)], local_sem=T.sem.ls)
        ls[0] += per * NB
    g.wait_ge(T.sem.ls, ls[0])


def rank_program(g, core, T, topo):
    pl = _plan(T, topo)
    rank = T.rank_of(core)
    if rank is not None:
        _rank_prog(g, core, T, topo, pl, rank)
    elif core in pl["cores"]:
        _compute_prog(g, core, T, topo, pl, pl["cores"].index(core))
    else:
        ls = [0]
        if core in pl["relay_of"]:
            _relay_prog(g, core, T, topo, pl, ls)
        if core in pl["rh_of"]:
            _scatter_prog(g, core, T, topo, pl, ls)
